import numpy as np
import ml_dtypes


def mxq(x, axis, fmt="e4m3"):
    dtype, down = {"e4m3": (ml_dtypes.float8_e4m3fn, 7), "e5m2": (ml_dtypes.float8_e5m2, 14)}[fmt]
    v = np.moveaxis(np.asarray(x, np.float32).astype(ml_dtypes.bfloat16).astype(np.float64), axis, -1)
    blocks = v.reshape(v.shape[:-1] + (-1, 32))
    amax = np.abs(blocks).max(-1, keepdims=True)
    byte = np.maximum(np.where(amax > 0, np.frexp(amax)[1] - 1 + 127, 0) - down, 1)
    scale = np.exp2(byte - 127.0)
    codes = (blocks / scale).astype(np.float32).astype(dtype).astype(np.float64)
    return np.moveaxis((codes * scale).reshape(v.shape), -1, axis)


WIDE = False


def mx_kscale(k):
    if not WIDE:
        return np.ones(k)
    levels = np.array([30, -30])
    if k % 512:
        return np.exp2(np.random.permutation(np.resize(levels, k // 32))).repeat(32)
    a = np.empty((k // 512, 16))
    for p in range(k // 512):
        a[p, :8] = np.random.permutation(np.resize(levels, 8))
        for g in range(8):
            far = levels[np.abs(levels - a[p, g]) >= 10]
            a[p, g + 8] = far[np.random.randint(len(far))]
    return np.exp2(a.ravel()).repeat(32)


def f64(x):
    return np.asarray(x).astype(np.float64)


def striped(idx):
    return np.tile(np.asarray(idx).reshape(-1, 16).T, (8, 1)).astype(np.uint16)


def unstriped(offs):
    return offs[:16].T.reshape(-1).astype(np.int64)


E2M1 = np.array([0.0, 0.5, 1.0, 1.5, 2.0, 3.0, 4.0, 6.0, -0.0, -0.5, -1.0, -1.5, -2.0, -3.0, -4.0, -6.0])


def pack_weight(w, fmt):
    k, n = w.shape
    w = f64(np.asarray(w, np.float32).astype(ml_dtypes.bfloat16)).reshape(k // 32, 32, n)
    amax = np.abs(w).max(1)
    if fmt in ("e4m3", "e5m2"):
        byte = np.frexp(amax)[1] - 1 + 127 - (7 if fmt == "e4m3" else 14)
    else:
        mant, ex = np.frexp(amax / 6.0)
        byte = np.where(mant > 0.5, ex, ex - 1) + 127
    byte = np.clip(np.where(amax > 0, byte, 1), 1, 254)
    scaled = (w * np.exp2(127.0 - byte)[:, None, :]).reshape(k, n).astype(np.float32)
    by_word = np.ascontiguousarray(scaled.reshape(k // 512, 128, 4, n).transpose(0, 1, 3, 2))
    if fmt in ("e4m3", "e5m2"):
        words = by_word.astype(ml_dtypes.float8_e4m3fn if fmt == "e4m3" else ml_dtypes.float8_e5m2).view(np.uint8)
    else:
        c = by_word.astype(ml_dtypes.float4_e2m1fn).view(np.uint8) & 0xF
        words = (c[..., 0::2] | (c[..., 1::2] << 4)).reshape(k // 512, 128, 2 * n)
    return np.ascontiguousarray(words), np.ascontiguousarray(byte.astype(np.uint8).reshape(k // 512, 16, n))


def unpack_weight(words, scales, fmt):
    g, _, n = scales.shape
    words = np.ascontiguousarray(words).reshape(g, 128, n, -1)
    if fmt in ("e4m3", "e5m2"):
        vals = words.view(ml_dtypes.float8_e4m3fn if fmt == "e4m3" else ml_dtypes.float8_e5m2).astype(np.float64)
    else:
        nib = np.empty((g, 128, n, 4), np.uint8)
        nib[..., 0::2] = words & 0xF
        nib[..., 1::2] = words >> 4
        vals = E2M1[nib]
    vals = vals * np.repeat(np.exp2(scales.astype(np.float64) - 127.0), 8, axis=1)[..., None]
    return vals.transpose(0, 1, 3, 2).reshape(g * 512, n)


def sigmoid(v):
    return 1.0 / (1.0 + np.exp(-v))


K, T, Z, J, R, Q, N = 512, 1024, 1024, 256, 512, 1024, 256


def setup_inputs():
    n = np.random.standard_normal
    idx = np.random.permutation(T)[:J]
    idx2 = np.random.permutation(Z)[:J]
    idx3 = np.random.permutation(Q)[:J]
    fk = mx_kscale(K)
    fr = mx_kscale(R)
    xtp = pack_weight(n((K, T)) / fk[:, None], "e5m2")
    xop = pack_weight(n((K, Z)) / fk[:, None], "e4m3")
    wp = pack_weight(n((K, R)) * 1 / np.sqrt(K) * fk[:, None] * fr, "e2m1")
    w2p = pack_weight(n((K, R)) * 1 / np.sqrt(K) * fk[:, None] * fr, "e5m2")
    wbp = pack_weight(n((R, N)) * 1 / np.sqrt(R) / fr[:, None], "e2m1")
    return {
        "xt_words": xtp[0],
        "xt_scales": xtp[1],
        "xo_words": xop[0],
        "xo_scales": xop[1],
        "w_words": wp[0],
        "w_scales": wp[1],
        "w2_words": w2p[0],
        "w2_scales": w2p[1],
        "tg": (1.0 * n((R, Q))).astype(np.float32),
        "sg": (np.random.uniform(0.6, 1.6, (R, 1))).astype(np.float32),
        "bg": (np.random.uniform(-1.0, 1.0, (R, 1))).astype(np.float32),
        "wb_words": wbp[0],
        "wb_scales": wbp[1],
        "offs": striped(idx),
        "offs2": striped(idx2),
        "offs3": striped(idx3),
    }


def reference(xt_words, xt_scales, xo_words, xo_scales, w_words, w_scales, w2_words, w2_scales, tg, sg, bg, wb_words, wb_scales, offs, offs2, offs3):
    idx = unstriped(offs)
    idx2 = unstriped(offs2)
    idx3 = unstriped(offs3)
    xtu = unpack_weight(xt_words, xt_scales, "e5m2")
    xou = unpack_weight(xo_words, xo_scales, "e4m3")
    wu = unpack_weight(w_words, w_scales, "e2m1")
    w2u = unpack_weight(w2_words, w2_scales, "e5m2")
    wbu = unpack_weight(wb_words, wb_scales, "e2m1")
    xtidxg = xtu[:, idx]
    xoidx2g = xou[:, idx2]
    a = wu.T @ xtidxg + w2u.T @ xoidx2g
    b = w2u.T @ xtidxg + wu.T @ xoidx2g
    hid = np.maximum(a, b) * sigmoid(f64(tg)[:, idx3] * f64(sg) + f64(bg))
    hidq = mxq(hid, 0, "e4m3")
    y = wbu.T @ hidq
    return y

@@ -1,0 +1,156 @@
+from contextlib import ExitStack
+
+import concourse.mybir as mybir
+from concourse.masks import make_identity
+
+K, T, J, R, Q, N = 512, 1024, 256, 512, 1024, 256
+FLOPS = 2 * (4 * K * R * J + R * N * J)
+
+F32 = mybir.dt.float32
+BF16 = mybir.dt.bfloat16
+I32 = mybir.dt.int32
+U32 = mybir.dt.uint32
+U16 = mybir.dt.uint16
+U8 = mybir.dt.uint8
+E4M3 = mybir.dt.float8_e4m3fn_x4
+E5M2 = mybir.dt.float8_e5m2_x4
+E2M1 = mybir.dt.float4_e2m1fn_x4
+ACT = mybir.ActivationFunctionType
+ALU = mybir.AluOpType
+
+P = 128
+PACK = 4
+ROWS = 16
+HALVES = J // P
+W_AT, W2_AT, WB_AT, XT_AT, XO_AT = 0, R, 2 * R, 2 * R + N, 2 * R + N + J
+SCALE_COLS = XO_AT + J
+
+
+def tile_list_crossed_tablegate_one_plain_kernel(
+    tc, xt_words, xt_scales, xo_words, xo_scales, w_words, w_scales, w2_words, w2_scales,
+    tg, sg, bg, wb_words, wb_scales, offs, offs2, offs3, out,
+):
+    nc = tc.nc
+    with ExitStack() as ctx:
+        lists = ctx.enter_context(tc.tile_pool(name="lists", bufs=1))
+        sb = ctx.enter_context(tc.tile_pool(name="sb", bufs=1))
+        ps = ctx.enter_context(tc.psum_pool(name="ps", bufs=1))
+
+        idx_t = lists.tile([P, J // 16], U16, name="idx_t")
+        idx_o = lists.tile([P, J // 16], U16, name="idx_o")
+        idx_g = lists.tile([P, J // 16], U16, name="idx_g")
+
+        xt_w = sb.tile([P, T], U32, name="xt_w", align_bytes=64)
+        xo_w = sb.tile([P, T], U32, name="xo_w", align_bytes=64)
+        xt_s = sb.tile([P, T], U8, name="xt_s", align_bytes=64)
+        xo_s = sb.tile([P, T], U8, name="xo_s", align_bytes=64)
+        w_w = sb.tile([P, 2 * R], U8, name="w_w", align_bytes=64)
+        w2_w = sb.tile([P, R], U32, name="w2_w", align_bytes=64)
+        wb_w = sb.tile([P, 2 * N], U8, name="wb_w", align_bytes=64)
+        scales = sb.tile([P, SCALE_COLS], U8, name="scales", align_bytes=64)
+        table = [sb.tile([P, Q], F32, name=f"table{t}") for t in range(PACK)]
+        slope = sb.tile([P, PACK], F32, name="slope")
+        offset = sb.tile([P, PACK], F32, name="offset")
+        ident = sb.tile([P, P], F32, name="ident")
+
+        nc.vector.memset(xt_s[:].bitcast(I32), 0)
+        nc.vector.memset(xo_s[:].bitcast(I32), 0)
+        nc.vector.memset(scales[:, 0:XT_AT].bitcast(I32), 0)
+
+        nc.sync.dma_start(idx_t[:], offs)
+        nc.sync.dma_start(idx_o[:], offs2)
+        nc.scalar.dma_start(xt_s[0:ROWS, :].bitcast(I32), xt_scales[0].bitcast(I32))
+        nc.scalar.dma_start(xo_s[0:ROWS, :].bitcast(I32), xo_scales[0].bitcast(I32))
+        nc.scalar.dma_start(scales[0:ROWS, W_AT : W_AT + R].bitcast(I32), w_scales[0].bitcast(I32))
+        nc.scalar.dma_start(scales[0:ROWS, W2_AT : W2_AT + R].bitcast(I32), w2_scales[0].bitcast(I32))
+        nc.scalar.dma_start(scales[0:ROWS, WB_AT : WB_AT + N].bitcast(I32), wb_scales[0].bitcast(I32))
+        nc.sync.dma_start(xt_w[:].bitcast(I32), xt_words[0].rearrange("p c b -> p (c b)").bitcast(I32))
+        nc.sync.dma_start(xo_w[:].bitcast(I32), xo_words[0].rearrange("p c b -> p (c b)").bitcast(I32))
+        nc.sync.dma_start(w_w[:].bitcast(I32), w_words[0].bitcast(I32))
+        nc.sync.dma_start(w2_w[:].bitcast(I32), w2_words[0].rearrange("p c b -> p (c b)").bitcast(I32))
+        nc.sync.dma_start(idx_g[:], offs3)
+        nc.sync.dma_start(wb_w[:].bitcast(I32), wb_words[0].bitcast(I32))
+        tg_rows = tg.rearrange("(p t) q -> t p q", t=PACK)
+        for t in range(PACK):
+            nc.sync.dma_start(table[t][:], tg_rows[t])
+        nc.gpsimd.dma_start(slope[:], sg.rearrange("(p t) o -> p (t o)", t=PACK))
+        nc.gpsimd.dma_start(offset[:], bg.rearrange("(p t) o -> p (t o)", t=PACK))
+        make_identity(nc, ident[:])
+
+        xt_gs = sb.tile([P, J], U8, name="xt_gs", align_bytes=64)
+        xo_gs = sb.tile([P, J], U8, name="xo_gs", align_bytes=64)
+        xt_gw = sb.tile([P, J], U32, name="xt_gw", align_bytes=64)
+        xo_gw = sb.tile([P, J], U32, name="xo_gw", align_bytes=64)
+        nc.vector.tensor_copy(xt_gs[:], xt_s[:].indirect(idx_t[:]))
+        nc.vector.tensor_copy(xo_gs[:], xo_s[:].indirect(idx_o[:]))
+        nc.vector.tensor_copy(scales[:, XT_AT : XT_AT + J].bitcast(I32), xt_gs[:].bitcast(I32))
+        nc.vector.tensor_copy(scales[:, XO_AT : XO_AT + J].bitcast(I32), xo_gs[:].bitcast(I32))
+        for quad in range(1, 4):
+            nc.scalar.dma_start(
+                scales[32 * quad : 32 * quad + 4, :].bitcast(I32), scales[4 * quad : 4 * quad + 4, :].bitcast(I32)
+            )
+        nc.vector.tensor_copy(xt_gw[:], xt_w[:].indirect(idx_t[:]))
+        nc.vector.tensor_copy(xo_gw[:], xo_w[:].indirect(idx_o[:]))
+
+        gate_first = sb.tile([P, PACK - 1, J], F32, name="gate_first")
+        gate_last = sb.tile([P, J], F32, name="gate_last")
+        gates = [gate_first[:, t, :] for t in range(PACK - 1)] + [gate_last[:]]
+
+        w_op = (w_w[:].bitcast(E2M1), scales[:, W_AT : W_AT + R])
+        w2_op = (w2_w[:].bitcast(E5M2), scales[:, W2_AT : W2_AT + R])
+        turned = []
+        for h in range(HALVES):
+            cols = slice(h * P, (h + 1) * P)
+            xt_op = (xt_gw[:, cols].bitcast(E5M2), scales[:, XT_AT + h * P : XT_AT + (h + 1) * P])
+            xo_op = (xo_gw[:, cols].bitcast(E4M3), scales[:, XO_AT + h * P : XO_AT + (h + 1) * P])
+            a_ps = ps.tile([P, R], F32, name=f"a_ps{h}")
+            b_ps = ps.tile([P, R], F32, name=f"b_ps{h}")
+            for acc, with_xt, with_xo in ((a_ps, w_op, w2_op), (b_ps, w2_op, w_op)):
+                nc.tensor.matmul_mx(acc[:], lhsT=xt_op[0], lhsT_scale=xt_op[1], rhs=with_xt[0], rhs_scale=with_xt[1], start=True, stop=False)
+                nc.tensor.matmul_mx(acc[:], lhsT=xo_op[0], lhsT_scale=xo_op[1], rhs=with_xo[0], rhs_scale=with_xo[1], start=False, stop=True)
+            a_sb = sb.tile([P, PACK, P], F32, name=f"a_sb{h}")
+            larger = sb.tile([P, PACK, P], F32, name=f"larger{h}")
+            nc.scalar.copy(a_sb[:], a_ps[:].rearrange("j (p t) -> j t p", t=PACK))
+            nc.vector.tensor_tensor(larger[:], b_ps[:].rearrange("j (p t) -> j t p", t=PACK), a_sb[:], ALU.max)
+            m_ps = ps.tile([P, PACK, P], F32, name=f"m_ps{h}")
+            for t in range(PACK):
+                nc.tensor.transpose(m_ps[:, t, :], larger[:, t, :], ident[:])
+            turned.append(m_ps)
+
+        for t in range(PACK):
+            nc.scalar.activation(
+                out=gates[t], in_=table[t][:].indirect(idx_g[:]), func=ACT.Sigmoid,
+                bias=offset[:, t : t + 1], scale=slope[:, t : t + 1],
+            )
+
+        hid = sb.tile([P, J, PACK], BF16, name="hid", align_bytes=64)
+        for h in range(HALVES):
+            cols = slice(h * P, (h + 1) * P)
+            nc.vector.tensor_tensor(
+                hid[:, cols, 0 : PACK - 1],
+                turned[h][:, 0 : PACK - 1, :].rearrange("p t j -> p j t"),
+                gate_first[:, :, cols].rearrange("p t j -> p j t"),
+                ALU.mult,
+            )
+        for h in range(HALVES):
+            cols = slice(h * P, (h + 1) * P)
+            nc.vector.tensor_tensor(hid[:, cols, PACK - 1], turned[h][:, PACK - 1, :], gate_last[:, cols], ALU.mult)
+
+        hid_w = sb.tile([P, J], U32, name="hid_w", align_bytes=64)
+        hid_s = sb.tile([P, J], U8, name="hid_s", align_bytes=64)
+        nc.vector.quantize_mx(hid_w[:].bitcast(E4M3), hid_s[:], hid[:].rearrange("p j t -> p (j t)"))
+
+        for h in range(N // P):
+            y_ps = ps.tile([P, J], F32, name=f"y_ps{h}")
+            nc.tensor.matmul_mx(
+                y_ps[:], lhsT=wb_w[:, 2 * h * P : 2 * (h + 1) * P].bitcast(E2M1),
+                lhsT_scale=scales[:, WB_AT + h * P : WB_AT + (h + 1) * P],
+                rhs=hid_w[:].bitcast(E4M3), rhs_scale=hid_s[:], start=True, stop=True,
+            )
+            y_sb = sb.tile([P, J], F32, name=f"y_sb{h}")
+            if h == 0:
+                nc.vector.tensor_copy(y_sb[:], y_ps[:])
+                nc.sync.dma_start(out[h * P : (h + 1) * P, :], y_sb[:])
+            else:
+                nc.scalar.copy(y_sb[:], y_ps[:])
+                nc.scalar.dma_start(out[h * P : (h + 1) * P, :], y_sb[:])

@@ -22,7 +22,7 @@ P = 128
 PACK = 4
 ROWS = 16
 HALVES = J // P
-W_AT, W2_AT, WB_AT, XT_AT, XO_AT = 0, R, 2 * R, 2 * R + N, 2 * R + N + J
+W_AT, W2_AT, XT_AT, XO_AT = 0, R, 2 * R, 2 * R + J
 SCALE_COLS = XO_AT + J
 
 
@@ -34,67 +34,76 @@ def tile_list_crossed_tablegate_one_plain_kernel(
     with ExitStack() as ctx:
         lists = ctx.enter_context(tc.tile_pool(name="lists", bufs=1))
         sb = ctx.enter_context(tc.tile_pool(name="sb", bufs=1))
+        shared = ctx.enter_context(tc.tile_pool(name="shared", bufs=1))
         ps = ctx.enter_context(tc.psum_pool(name="ps", bufs=1))
 
         idx_t = lists.tile([P, J // 16], U16, name="idx_t")
         idx_o = lists.tile([P, J // 16], U16, name="idx_o")
         idx_g = lists.tile([P, J // 16], U16, name="idx_g")
 
-        xt_w = sb.tile([P, T], U32, name="xt_w", align_bytes=64)
-        xo_w = sb.tile([P, T], U32, name="xo_w", align_bytes=64)
+        xt_w = sb.tile([P, T], U32, name="xt_w", tag="buf1", align_bytes=64)
+        xo_w = sb.tile([P, T], U32, name="xo_w", tag="buf2", align_bytes=64)
         xt_s = sb.tile([P, T], U8, name="xt_s", align_bytes=64)
         xo_s = sb.tile([P, T], U8, name="xo_s", align_bytes=64)
         w_w = sb.tile([P, 2 * R], U8, name="w_w", align_bytes=64)
         w2_w = sb.tile([P, R], U32, name="w2_w", align_bytes=64)
         wb_w = sb.tile([P, 2 * N], U8, name="wb_w", align_bytes=64)
         scales = sb.tile([P, SCALE_COLS], U8, name="scales", align_bytes=64)
-        table = [sb.tile([P, Q], F32, name=f"table{t}") for t in range(PACK)]
+        staged = sb.tile([ROWS, SCALE_COLS], U8, name="staged", tag="buf3", align_bytes=64)
+        wb_s = sb.tile([P, N], U8, name="wb_s", align_bytes=64)
+        table = [sb.tile([P, Q], F32, name="table0", tag="buf0", align_bytes=64)]
         slope = sb.tile([P, PACK], F32, name="slope")
         offset = sb.tile([P, PACK], F32, name="offset")
         ident = sb.tile([P, P], F32, name="ident")
 
-        nc.vector.memset(xt_s[:].bitcast(I32), 0)
         nc.vector.memset(xo_s[:].bitcast(I32), 0)
-        nc.vector.memset(scales[:, 0:XT_AT].bitcast(I32), 0)
+        nc.vector.memset(xt_s[:].bitcast(I32), 0)
+        nc.vector.memset(scales[:].bitcast(I32), 0)
+        nc.vector.memset(wb_s[:].bitcast(I32), 0)
 
-        nc.sync.dma_start(idx_t[:], offs)
+        tg_rows = tg.rearrange("(p t) q -> t p q", t=PACK)
         nc.sync.dma_start(idx_o[:], offs2)
+        nc.sync.dma_start(idx_t[:], offs)
         nc.scalar.dma_start(xt_s[0:ROWS, :].bitcast(I32), xt_scales[0].bitcast(I32))
-        nc.scalar.dma_start(xo_s[0:ROWS, :].bitcast(I32), xo_scales[0].bitcast(I32))
-        nc.scalar.dma_start(scales[0:ROWS, W_AT : W_AT + R].bitcast(I32), w_scales[0].bitcast(I32))
-        nc.scalar.dma_start(scales[0:ROWS, W2_AT : W2_AT + R].bitcast(I32), w2_scales[0].bitcast(I32))
-        nc.scalar.dma_start(scales[0:ROWS, WB_AT : WB_AT + N].bitcast(I32), wb_scales[0].bitcast(I32))
+        nc.sync.dma_start(staged[:, W_AT : W_AT + R].bitcast(I32), w_scales[0].bitcast(I32))
+        nc.sync.dma_start(xo_s[0:ROWS, :].bitcast(I32), xo_scales[0].bitcast(I32))
+        nc.sync.dma_start(staged[:, W2_AT : W2_AT + R].bitcast(I32), w2_scales[0].bitcast(I32))
+        nc.sync.dma_start(idx_g[:], offs3)
         nc.sync.dma_start(xt_w[:].bitcast(I32), xt_words[0].rearrange("p c b -> p (c b)").bitcast(I32))
         nc.sync.dma_start(xo_w[:].bitcast(I32), xo_words[0].rearrange("p c b -> p (c b)").bitcast(I32))
         nc.sync.dma_start(w_w[:].bitcast(I32), w_words[0].bitcast(I32))
         nc.sync.dma_start(w2_w[:].bitcast(I32), w2_words[0].rearrange("p c b -> p (c b)").bitcast(I32))
-        nc.sync.dma_start(idx_g[:], offs3)
-        nc.sync.dma_start(wb_w[:].bitcast(I32), wb_words[0].bitcast(I32))
-        tg_rows = tg.rearrange("(p t) q -> t p q", t=PACK)
-        for t in range(PACK):
-            nc.sync.dma_start(table[t][:], tg_rows[t])
+        nc.sync.dma_start(table[0][:], tg_rows[0])
         nc.gpsimd.dma_start(slope[:], sg.rearrange("(p t) o -> p (t o)", t=PACK))
         nc.gpsimd.dma_start(offset[:], bg.rearrange("(p t) o -> p (t o)", t=PACK))
         make_identity(nc, ident[:])
 
         xt_gs = sb.tile([P, J], U8, name="xt_gs", align_bytes=64)
-        xo_gs = sb.tile([P, J], U8, name="xo_gs", align_bytes=64)
-        xt_gw = sb.tile([P, J], U32, name="xt_gw", align_bytes=64)
-        xo_gw = sb.tile([P, J], U32, name="xo_gw", align_bytes=64)
+        xo_gs = shared.tile([P, J], U8, name="xo_gs", align_bytes=64, offset=4 * J - J // 2)
+        xt_gw = shared.tile([P, J], U32, name="xt_gw", align_bytes=64, offset=0)
+        xo_gw = shared.tile([P, J], U32, name="xo_gw", align_bytes=64, offset=4 * J)
         nc.vector.tensor_copy(xt_gs[:], xt_s[:].indirect(idx_t[:]))
         nc.vector.tensor_copy(xo_gs[:], xo_s[:].indirect(idx_o[:]))
-        nc.vector.tensor_copy(scales[:, XT_AT : XT_AT + J].bitcast(I32), xt_gs[:].bitcast(I32))
-        nc.vector.tensor_copy(scales[:, XO_AT : XO_AT + J].bitcast(I32), xo_gs[:].bitcast(I32))
+        nc.vector.tensor_copy(staged[:, XT_AT : XT_AT + J].bitcast(I32), xt_gs[0:ROWS, :].bitcast(I32))
+        nc.vector.tensor_copy(staged[:, XO_AT : XO_AT + J].bitcast(I32), xo_gs[0:ROWS, :].bitcast(I32))
         for quad in range(1, 4):
             nc.scalar.dma_start(
-                scales[32 * quad : 32 * quad + 4, :].bitcast(I32), scales[4 * quad : 4 * quad + 4, :].bitcast(I32)
+                scales[32 * quad : 32 * quad + 4, :].bitcast(I32), staged[4 * quad : 4 * quad + 4, :].bitcast(I32)
             )
+        nc.vector.tensor_copy(scales[0:4, :].bitcast(I32), staged[0:4, :].bitcast(I32))
         nc.vector.tensor_copy(xt_gw[:], xt_w[:].indirect(idx_t[:]))
         nc.vector.tensor_copy(xo_gw[:], xo_w[:].indirect(idx_o[:]))
 
-        gate_first = sb.tile([P, PACK - 1, J], F32, name="gate_first")
-        gate_last = sb.tile([P, J], F32, name="gate_last")
-        gates = [gate_first[:, t, :] for t in range(PACK - 1)] + [gate_last[:]]
+        for t in range(1, PACK):
+            table.append(sb.tile([P, Q], F32, name=f"table{t}", tag=f"buf{t}", align_bytes=64))
+            nc.sync.dma_start(table[t][:], tg_rows[t])
+        nc.sync.dma_start(wb_w[:].bitcast(I32), wb_words[0].bitcast(I32))
+        for quad in range(4):
+            nc.sync.dma_start(
+                wb_s[32 * quad : 32 * quad + 4, :].bitcast(I32), wb_scales[0, 4 * quad : 4 * quad + 4, :].bitcast(I32)
+            )
+
+        gate = sb.tile([P, PACK, J], F32, name="gate")
 
         w_op = (w_w[:].bitcast(E2M1), scales[:, W_AT : W_AT + R])
         w2_op = (w2_w[:].bitcast(E5M2), scales[:, W2_AT : W2_AT + R])
@@ -110,7 +119,7 @@ def tile_list_crossed_tablegate_one_plain_kernel(
                 nc.tensor.matmul_mx(acc[:], lhsT=xo_op[0], lhsT_scale=xo_op[1], rhs=with_xo[0], rhs_scale=with_xo[1], start=False, stop=True)
             a_sb = sb.tile([P, PACK, P], F32, name=f"a_sb{h}")
             larger = sb.tile([P, PACK, P], F32, name=f"larger{h}")
-            nc.scalar.copy(a_sb[:], a_ps[:].rearrange("j (p t) -> j t p", t=PACK))
+            nc.vector.tensor_copy(a_sb[:], a_ps[:].rearrange("j (p t) -> j t p", t=PACK))
             nc.vector.tensor_tensor(larger[:], b_ps[:].rearrange("j (p t) -> j t p", t=PACK), a_sb[:], ALU.max)
             m_ps = ps.tile([P, PACK, P], F32, name=f"m_ps{h}")
             for t in range(PACK):
@@ -119,38 +128,33 @@ def tile_list_crossed_tablegate_one_plain_kernel(
 
         for t in range(PACK):
             nc.scalar.activation(
-                out=gates[t], in_=table[t][:].indirect(idx_g[:]), func=ACT.Sigmoid,
+                out=gate[:, t, :], in_=table[t][:].indirect(idx_g[:]), func=ACT.Sigmoid,
                 bias=offset[:, t : t + 1], scale=slope[:, t : t + 1],
             )
 
-        hid = sb.tile([P, J, PACK], BF16, name="hid", align_bytes=64)
         for h in range(HALVES):
             cols = slice(h * P, (h + 1) * P)
+            hid = sb.tile([P, P, PACK], BF16, name=f"hid{h}", align_bytes=64)
             nc.vector.tensor_tensor(
-                hid[:, cols, 0 : PACK - 1],
-                turned[h][:, 0 : PACK - 1, :].rearrange("p t j -> p j t"),
-                gate_first[:, :, cols].rearrange("p t j -> p j t"),
-                ALU.mult,
+                hid[:], turned[h][:].rearrange("p t j -> p j t"), gate[:, :, cols].rearrange("p t j -> p j t"), ALU.mult
             )
-        for h in range(HALVES):
-            cols = slice(h * P, (h + 1) * P)
-            nc.vector.tensor_tensor(hid[:, cols, PACK - 1], turned[h][:, PACK - 1, :], gate_last[:, cols], ALU.mult)
-
-        hid_w = sb.tile([P, J], U32, name="hid_w", align_bytes=64)
-        hid_s = sb.tile([P, J], U8, name="hid_s", align_bytes=64)
-        nc.vector.quantize_mx(hid_w[:].bitcast(E4M3), hid_s[:], hid[:].rearrange("p j t -> p (j t)"))
-
-        for h in range(N // P):
-            y_ps = ps.tile([P, J], F32, name=f"y_ps{h}")
-            nc.tensor.matmul_mx(
-                y_ps[:], lhsT=wb_w[:, 2 * h * P : 2 * (h + 1) * P].bitcast(E2M1),
-                lhsT_scale=scales[:, WB_AT + h * P : WB_AT + (h + 1) * P],
-                rhs=hid_w[:].bitcast(E4M3), rhs_scale=hid_s[:], start=True, stop=True,
-            )
-            y_sb = sb.tile([P, J], F32, name=f"y_sb{h}")
-            if h == 0:
-                nc.vector.tensor_copy(y_sb[:], y_ps[:])
-                nc.sync.dma_start(out[h * P : (h + 1) * P, :], y_sb[:])
-            else:
-                nc.scalar.copy(y_sb[:], y_ps[:])
-                nc.scalar.dma_start(out[h * P : (h + 1) * P, :], y_sb[:])
+            hid_w = sb.tile([P, P], U32, name=f"hid_w{h}", align_bytes=64)
+            hid_s = sb.tile([P, P], U8, name=f"hid_s{h}", align_bytes=64)
+            nc.vector.quantize_mx(hid_w[:].bitcast(E4M3), hid_s[:], hid[:].rearrange("p j t -> p (j t)"))
+            for g in range(N // P):
+                y_ps = ps.tile([P, P], F32, name=f"y_ps{h}{g}", tag=f"y_ps{g}")
+                nc.tensor.matmul_mx(
+                    y_ps[:], lhsT=wb_w[:, 2 * g * P : 2 * (g + 1) * P].bitcast(E2M1),
+                    lhsT_scale=wb_s[:, g * P : (g + 1) * P],
+                    rhs=hid_w[:].bitcast(E4M3), rhs_scale=hid_s[:], start=True, stop=True,
+                )
+                y_sb = sb.tile([P, P], F32, name=f"y_sb{h}{g}")
+                if h == HALVES - 1 and g == 0:
+                    nc.vector.tensor_copy(y_sb[:], y_ps[:])
+                    nc.sync.dma_start(out[g * P : (g + 1) * P, cols], y_sb[:])
+                elif h == HALVES - 1:
+                    nc.scalar.copy(y_sb[:], y_ps[:])
+                    nc.scalar.dma_start(out[g * P : (g + 1) * P, cols], y_sb[:])
+                else:
+                    nc.scalar.copy(y_sb[:], y_ps[:])
+                    nc.sync.dma_start(out[g * P : (g + 1) * P, cols], y_sb[:])

@@ -22,8 +22,8 @@ P = 128
 PACK = 4
 ROWS = 16
 HALVES = J // P
-W_AT, W2_AT, XT_AT, XO_AT = 0, R, 2 * R, 2 * R + J
-SCALE_COLS = XO_AT + J
+W_AT, W2_AT, XT_AT = 0, R, 2 * R
+SCALE_COLS = XT_AT + J
 
 
 def tile_list_crossed_tablegate_one_plain_kernel(
@@ -34,68 +34,72 @@ def tile_list_crossed_tablegate_one_plain_kernel(
     with ExitStack() as ctx:
         lists = ctx.enter_context(tc.tile_pool(name="lists", bufs=1))
         sb = ctx.enter_context(tc.tile_pool(name="sb", bufs=1))
-        shared = ctx.enter_context(tc.tile_pool(name="shared", bufs=1))
         ps = ctx.enter_context(tc.psum_pool(name="ps", bufs=1))
 
         idx_t = lists.tile([P, J // 16], U16, name="idx_t")
         idx_o = lists.tile([P, J // 16], U16, name="idx_o")
         idx_g = lists.tile([P, J // 16], U16, name="idx_g")
 
-        xt_w = sb.tile([P, T], U32, name="xt_w", tag="buf1", align_bytes=64)
-        xo_w = sb.tile([P, T], U32, name="xo_w", tag="buf2", align_bytes=64)
+        xt_w = sb.tile([P, T], U32, name="xt_w", align_bytes=64)
+        xo_w = sb.tile([P, T], U32, name="xo_w", align_bytes=64)
         xt_s = sb.tile([P, T], U8, name="xt_s", align_bytes=64)
         xo_s = sb.tile([P, T], U8, name="xo_s", align_bytes=64)
         w_w = sb.tile([P, 2 * R], U8, name="w_w", align_bytes=64)
         w2_w = sb.tile([P, R], U32, name="w2_w", align_bytes=64)
         wb_w = sb.tile([P, 2 * N], U8, name="wb_w", align_bytes=64)
         scales = sb.tile([P, SCALE_COLS], U8, name="scales", align_bytes=64)
-        staged = sb.tile([ROWS, SCALE_COLS], U8, name="staged", tag="buf3", align_bytes=64)
+        staged = sb.tile([ROWS, SCALE_COLS], U8, name="staged", align_bytes=64)
+        xo_p = sb.tile([P, J], U8, name="xo_p", align_bytes=64)
         wb_s = sb.tile([P, N], U8, name="wb_s", align_bytes=64)
-        table = [sb.tile([P, Q], F32, name="table0", tag="buf0", align_bytes=64)]
+        table = [sb.tile([P, Q], F32, name=f"table{t}") for t in range(PACK)]
         slope = sb.tile([P, PACK], F32, name="slope")
         offset = sb.tile([P, PACK], F32, name="offset")
         ident = sb.tile([P, P], F32, name="ident")
 
-        nc.vector.memset(xo_s[:].bitcast(I32), 0)
         nc.vector.memset(xt_s[:].bitcast(I32), 0)
+        nc.gpsimd.memset(xo_s[:].bitcast(I32), 0)
         nc.vector.memset(scales[:].bitcast(I32), 0)
+        nc.vector.memset(xo_p[:].bitcast(I32), 0)
         nc.vector.memset(wb_s[:].bitcast(I32), 0)
 
         tg_rows = tg.rearrange("(p t) q -> t p q", t=PACK)
-        nc.sync.dma_start(idx_o[:], offs2)
         nc.sync.dma_start(idx_t[:], offs)
         nc.scalar.dma_start(xt_s[0:ROWS, :].bitcast(I32), xt_scales[0].bitcast(I32))
+        nc.sync.dma_start(idx_o[:], offs2)
         nc.sync.dma_start(staged[:, W_AT : W_AT + R].bitcast(I32), w_scales[0].bitcast(I32))
-        nc.sync.dma_start(xo_s[0:ROWS, :].bitcast(I32), xo_scales[0].bitcast(I32))
         nc.sync.dma_start(staged[:, W2_AT : W2_AT + R].bitcast(I32), w2_scales[0].bitcast(I32))
-        nc.sync.dma_start(idx_g[:], offs3)
-        nc.sync.dma_start(xt_w[:].bitcast(I32), xt_words[0].rearrange("p c b -> p (c b)").bitcast(I32))
-        nc.sync.dma_start(xo_w[:].bitcast(I32), xo_words[0].rearrange("p c b -> p (c b)").bitcast(I32))
-        nc.sync.dma_start(w_w[:].bitcast(I32), w_words[0].bitcast(I32))
+        nc.sync.dma_start(xo_s[0:ROWS, :].bitcast(I32), xo_scales[0].bitcast(I32))
         nc.sync.dma_start(w2_w[:].bitcast(I32), w2_words[0].rearrange("p c b -> p (c b)").bitcast(I32))
-        nc.sync.dma_start(table[0][:], tg_rows[0])
+        nc.sync.dma_start(xt_w[:].bitcast(I32), xt_words[0].rearrange("p c b -> p (c b)").bitcast(I32))
+        nc.sync.dma_start(w_w[:].bitcast(I32), w_words[0].bitcast(I32))
+        nc.sync.dma_start(idx_g[:], offs3)
+        nc.sync.dma_start(xo_w[:].bitcast(I32), xo_words[0].rearrange("p c b -> p (c b)").bitcast(I32))
         nc.gpsimd.dma_start(slope[:], sg.rearrange("(p t) o -> p (t o)", t=PACK))
         nc.gpsimd.dma_start(offset[:], bg.rearrange("(p t) o -> p (t o)", t=PACK))
         make_identity(nc, ident[:])
 
-        xt_gs = sb.tile([P, J], U8, name="xt_gs", align_bytes=64)
-        xo_gs = shared.tile([P, J], U8, name="xo_gs", align_bytes=64, offset=4 * J - J // 2)
-        xt_gw = shared.tile([P, J], U32, name="xt_gw", align_bytes=64, offset=0)
-        xo_gw = shared.tile([P, J], U32, name="xo_gw", align_bytes=64, offset=4 * J)
+        xt_gs = sb.tile([P, J], U8, name="xt_gs", tag="gathered_scales", align_bytes=64)
         nc.vector.tensor_copy(xt_gs[:], xt_s[:].indirect(idx_t[:]))
-        nc.vector.tensor_copy(xo_gs[:], xo_s[:].indirect(idx_o[:]))
-        nc.vector.tensor_copy(staged[:, XT_AT : XT_AT + J].bitcast(I32), xt_gs[0:ROWS, :].bitcast(I32))
-        nc.vector.tensor_copy(staged[:, XO_AT : XO_AT + J].bitcast(I32), xo_gs[0:ROWS, :].bitcast(I32))
+        nc.vector.tensor_copy(staged[:, XT_AT:SCALE_COLS].bitcast(I32), xt_gs[0:ROWS, :].bitcast(I32))
         for quad in range(1, 4):
-            nc.scalar.dma_start(
+            nc.sync.dma_start(
                 scales[32 * quad : 32 * quad + 4, :].bitcast(I32), staged[4 * quad : 4 * quad + 4, :].bitcast(I32)
             )
-        nc.vector.tensor_copy(scales[0:4, :].bitcast(I32), staged[0:4, :].bitcast(I32))
+        nc.sync.dma_start(table[0][:], tg_rows[0])
+        xo_gs = sb.tile([P, J], U8, name="xo_gs", tag="gathered_scales", align_bytes=64)
+        nc.vector.tensor_copy(xo_gs[:], xo_s[:].indirect(idx_o[:]))
+        for quad in range(1, 4):
+            nc.sync.dma_start(
+                xo_p[32 * quad : 32 * quad + 4, :].bitcast(I32), xo_gs[4 * quad : 4 * quad + 4, :].bitcast(I32)
+            )
+        xt_gw = sb.tile([P, J], U32, name="xt_gw", align_bytes=64)
+        xo_gw = sb.tile([P, J], U32, name="xo_gw", align_bytes=64)
         nc.vector.tensor_copy(xt_gw[:], xt_w[:].indirect(idx_t[:]))
+        nc.vector.tensor_copy(scales[0:4, :].bitcast(I32), staged[0:4, :].bitcast(I32))
+        nc.vector.tensor_copy(xo_p[0:4, :].bitcast(I32), xo_gs[0:4, :].bitcast(I32))
         nc.vector.tensor_copy(xo_gw[:], xo_w[:].indirect(idx_o[:]))
 
         for t in range(1, PACK):
-            table.append(sb.tile([P, Q], F32, name=f"table{t}", tag=f"buf{t}", align_bytes=64))
             nc.sync.dma_start(table[t][:], tg_rows[t])
         nc.sync.dma_start(wb_w[:].bitcast(I32), wb_words[0].bitcast(I32))
         for quad in range(4):
@@ -107,23 +111,28 @@ def tile_list_crossed_tablegate_one_plain_kernel(
 
         w_op = (w_w[:].bitcast(E2M1), scales[:, W_AT : W_AT + R])
         w2_op = (w2_w[:].bitcast(E5M2), scales[:, W2_AT : W2_AT + R])
-        turned = []
+        maxima, turned = [], []
         for h in range(HALVES):
             cols = slice(h * P, (h + 1) * P)
             xt_op = (xt_gw[:, cols].bitcast(E5M2), scales[:, XT_AT + h * P : XT_AT + (h + 1) * P])
-            xo_op = (xo_gw[:, cols].bitcast(E4M3), scales[:, XO_AT + h * P : XO_AT + (h + 1) * P])
-            a_ps = ps.tile([P, R], F32, name=f"a_ps{h}")
+            xo_op = (xo_gw[:, cols].bitcast(E4M3), xo_p[:, cols])
+            a_ps = ps.tile([P, R], F32, name=f"a_ps{h}", tag=f"a_then_turned{h}")
             b_ps = ps.tile([P, R], F32, name=f"b_ps{h}")
-            for acc, with_xt, with_xo in ((a_ps, w_op, w2_op), (b_ps, w2_op, w_op)):
-                nc.tensor.matmul_mx(acc[:], lhsT=xt_op[0], lhsT_scale=xt_op[1], rhs=with_xt[0], rhs_scale=with_xt[1], start=True, stop=False)
-                nc.tensor.matmul_mx(acc[:], lhsT=xo_op[0], lhsT_scale=xo_op[1], rhs=with_xo[0], rhs_scale=with_xo[1], start=False, stop=True)
+            passes = [(a_ps, xt_op, w_op), (b_ps, xt_op, w2_op), (a_ps, xo_op, w2_op), (b_ps, xo_op, w_op)]
+            for i in ((0, 1, 2, 3) if h == 0 else (0, 2, 1, 3)):
+                acc, x_op, weight = passes[i]
+                nc.tensor.matmul_mx(
+                    acc[:], lhsT=x_op[0], lhsT_scale=x_op[1], rhs=weight[0], rhs_scale=weight[1], start=i < 2, stop=i >= 2
+                )
             a_sb = sb.tile([P, PACK, P], F32, name=f"a_sb{h}")
             larger = sb.tile([P, PACK, P], F32, name=f"larger{h}")
             nc.vector.tensor_copy(a_sb[:], a_ps[:].rearrange("j (p t) -> j t p", t=PACK))
             nc.vector.tensor_tensor(larger[:], b_ps[:].rearrange("j (p t) -> j t p", t=PACK), a_sb[:], ALU.max)
-            m_ps = ps.tile([P, PACK, P], F32, name=f"m_ps{h}")
+            maxima.append(larger)
+        for h in range(HALVES):
+            m_ps = ps.tile([P, PACK, P], F32, name=f"m_ps{h}", tag=f"a_then_turned{1 - h}")
             for t in range(PACK):
-                nc.tensor.transpose(m_ps[:, t, :], larger[:, t, :], ident[:])
+                nc.tensor.transpose(m_ps[:, t, :], maxima[h][:, t, :], ident[:])
             turned.append(m_ps)
 
         for t in range(PACK):
@@ -142,7 +151,7 @@ def tile_list_crossed_tablegate_one_plain_kernel(
             hid_s = sb.tile([P, P], U8, name=f"hid_s{h}", align_bytes=64)
             nc.vector.quantize_mx(hid_w[:].bitcast(E4M3), hid_s[:], hid[:].rearrange("p j t -> p (j t)"))
             for g in range(N // P):
-                y_ps = ps.tile([P, P], F32, name=f"y_ps{h}{g}", tag=f"y_ps{g}")
+                y_ps = ps.tile([P, P], F32, name=f"y_ps{h}{g}", tag=f"y_ps{h}{g}")
                 nc.tensor.matmul_mx(
                     y_ps[:], lhsT=wb_w[:, 2 * g * P : 2 * (g + 1) * P].bitcast(E2M1),
                     lhsT_scale=wb_s[:, g * P : (g + 1) * P],

from contextlib import ExitStack

import concourse.mybir as mybir
from concourse.masks import make_identity

K, T, J, R, Q, N = 512, 1024, 256, 512, 1024, 256
FLOPS = 2 * (4 * K * R * J + R * N * J)

F32 = mybir.dt.float32
BF16 = mybir.dt.bfloat16
I32 = mybir.dt.int32
U32 = mybir.dt.uint32
U16 = mybir.dt.uint16
U8 = mybir.dt.uint8
E4M3 = mybir.dt.float8_e4m3fn_x4
E5M2 = mybir.dt.float8_e5m2_x4
E2M1 = mybir.dt.float4_e2m1fn_x4
ACT = mybir.ActivationFunctionType
ALU = mybir.AluOpType

P = 128
PACK = 4
ROWS = 16
HALVES = J // P
W_AT, W2_AT, XT_AT = 0, R, 2 * R
SCALE_COLS = XT_AT + J


def tile_list_crossed_tablegate_one_plain_kernel(
    tc, xt_words, xt_scales, xo_words, xo_scales, w_words, w_scales, w2_words, w2_scales,
    tg, sg, bg, wb_words, wb_scales, offs, offs2, offs3, out,
):
    nc = tc.nc
    with ExitStack() as ctx:
        lists = ctx.enter_context(tc.tile_pool(name="lists", bufs=1))
        sb = ctx.enter_context(tc.tile_pool(name="sb", bufs=1))
        ps = ctx.enter_context(tc.psum_pool(name="ps", bufs=1))

        idx_t = lists.tile([P, J // 16], U16, name="idx_t")
        idx_o = lists.tile([P, J // 16], U16, name="idx_o")
        idx_g = lists.tile([P, J // 16], U16, name="idx_g")

        xt_w = sb.tile([P, T], U32, name="xt_w", align_bytes=64)
        xo_w = sb.tile([P, T], U32, name="xo_w", align_bytes=64)
        xt_s = sb.tile([P, T], U8, name="xt_s", align_bytes=64)
        xo_s = sb.tile([P, T], U8, name="xo_s", align_bytes=64)
        w_w = sb.tile([P, 2 * R], U8, name="w_w", align_bytes=64)
        w2_w = sb.tile([P, R], U32, name="w2_w", align_bytes=64)
        wb_w = sb.tile([P, 2 * N], U8, name="wb_w", align_bytes=64)
        scales = sb.tile([P, SCALE_COLS], U8, name="scales", align_bytes=64)
        staged = sb.tile([ROWS, SCALE_COLS], U8, name="staged", align_bytes=64)
        xo_p = sb.tile([P, J], U8, name="xo_p", align_bytes=64)
        wb_s = sb.tile([P, N], U8, name="wb_s", align_bytes=64)
        table = [sb.tile([P, Q], F32, name=f"table{t}") for t in range(PACK)]
        slope = sb.tile([P, PACK], F32, name="slope")
        offset = sb.tile([P, PACK], F32, name="offset")
        ident = sb.tile([P, P], F32, name="ident")

        nc.vector.memset(xt_s[:].bitcast(I32), 0)
        nc.gpsimd.memset(xo_s[:].bitcast(I32), 0)
        nc.vector.memset(scales[:].bitcast(I32), 0)
        nc.vector.memset(xo_p[:].bitcast(I32), 0)
        nc.vector.memset(wb_s[:].bitcast(I32), 0)

        tg_rows = tg.rearrange("(p t) q -> t p q", t=PACK)
        nc.sync.dma_start(idx_t[:], offs)
        nc.scalar.dma_start(xt_s[0:ROWS, :].bitcast(I32), xt_scales[0].bitcast(I32))
        nc.sync.dma_start(idx_o[:], offs2)
        nc.sync.dma_start(staged[:, W_AT : W_AT + R].bitcast(I32), w_scales[0].bitcast(I32))
        nc.sync.dma_start(staged[:, W2_AT : W2_AT + R].bitcast(I32), w2_scales[0].bitcast(I32))
        nc.sync.dma_start(xo_s[0:ROWS, :].bitcast(I32), xo_scales[0].bitcast(I32))
        nc.sync.dma_start(w2_w[:].bitcast(I32), w2_words[0].rearrange("p c b -> p (c b)").bitcast(I32))
        nc.sync.dma_start(xt_w[:].bitcast(I32), xt_words[0].rearrange("p c b -> p (c b)").bitcast(I32))
        nc.sync.dma_start(w_w[:].bitcast(I32), w_words[0].bitcast(I32))
        nc.sync.dma_start(idx_g[:], offs3)
        nc.sync.dma_start(xo_w[:].bitcast(I32), xo_words[0].rearrange("p c b -> p (c b)").bitcast(I32))
        nc.gpsimd.dma_start(slope[:], sg.rearrange("(p t) o -> p (t o)", t=PACK))
        nc.gpsimd.dma_start(offset[:], bg.rearrange("(p t) o -> p (t o)", t=PACK))
        make_identity(nc, ident[:])

        xt_gs = sb.tile([P, J], U8, name="xt_gs", tag="gathered_scales", align_bytes=64)
        nc.vector.tensor_copy(xt_gs[:], xt_s[:].indirect(idx_t[:]))
        nc.vector.tensor_copy(staged[:, XT_AT:SCALE_COLS].bitcast(I32), xt_gs[0:ROWS, :].bitcast(I32))
        for quad in range(1, 4):
            nc.sync.dma_start(
                scales[32 * quad : 32 * quad + 4, :].bitcast(I32), staged[4 * quad : 4 * quad + 4, :].bitcast(I32)
            )
        nc.sync.dma_start(table[0][:], tg_rows[0])
        xo_gs = sb.tile([P, J], U8, name="xo_gs", tag="gathered_scales", align_bytes=64)
        nc.vector.tensor_copy(xo_gs[:], xo_s[:].indirect(idx_o[:]))
        for quad in range(1, 4):
            nc.sync.dma_start(
                xo_p[32 * quad : 32 * quad + 4, :].bitcast(I32), xo_gs[4 * quad : 4 * quad + 4, :].bitcast(I32)
            )
        xt_gw = sb.tile([P, J], U32, name="xt_gw", align_bytes=64)
        xo_gw = sb.tile([P, J], U32, name="xo_gw", align_bytes=64)
        nc.vector.tensor_copy(xt_gw[:], xt_w[:].indirect(idx_t[:]))
        nc.vector.tensor_copy(scales[0:4, :].bitcast(I32), staged[0:4, :].bitcast(I32))
        nc.vector.tensor_copy(xo_p[0:4, :].bitcast(I32), xo_gs[0:4, :].bitcast(I32))
        nc.vector.tensor_copy(xo_gw[:], xo_w[:].indirect(idx_o[:]))

        for t in range(1, PACK):
            nc.sync.dma_start(table[t][:], tg_rows[t])
        nc.sync.dma_start(wb_w[:].bitcast(I32), wb_words[0].bitcast(I32))
        for quad in range(4):
            nc.sync.dma_start(
                wb_s[32 * quad : 32 * quad + 4, :].bitcast(I32), wb_scales[0, 4 * quad : 4 * quad + 4, :].bitcast(I32)
            )

        gate = sb.tile([P, PACK, J], F32, name="gate")

        w_op = (w_w[:].bitcast(E2M1), scales[:, W_AT : W_AT + R])
        w2_op = (w2_w[:].bitcast(E5M2), scales[:, W2_AT : W2_AT + R])
        maxima, turned = [], []
        for h in range(HALVES):
            cols = slice(h * P, (h + 1) * P)
            xt_op = (xt_gw[:, cols].bitcast(E5M2), scales[:, XT_AT + h * P : XT_AT + (h + 1) * P])
            xo_op = (xo_gw[:, cols].bitcast(E4M3), xo_p[:, cols])
            a_ps = ps.tile([P, R], F32, name=f"a_ps{h}", tag=f"a_then_turned{h}")
            b_ps = ps.tile([P, R], F32, name=f"b_ps{h}")
            passes = [(a_ps, xt_op, w_op), (b_ps, xt_op, w2_op), (a_ps, xo_op, w2_op), (b_ps, xo_op, w_op)]
            for i in ((0, 1, 2, 3) if h == 0 else (0, 2, 1, 3)):
                acc, x_op, weight = passes[i]
                nc.tensor.matmul_mx(
                    acc[:], lhsT=x_op[0], lhsT_scale=x_op[1], rhs=weight[0], rhs_scale=weight[1], start=i < 2, stop=i >= 2
                )
            a_sb = sb.tile([P, PACK, P], F32, name=f"a_sb{h}")
            larger = sb.tile([P, PACK, P], F32, name=f"larger{h}")
            nc.vector.tensor_copy(a_sb[:], a_ps[:].rearrange("j (p t) -> j t p", t=PACK))
            nc.vector.tensor_tensor(larger[:], b_ps[:].rearrange("j (p t) -> j t p", t=PACK), a_sb[:], ALU.max)
            maxima.append(larger)
        for h in range(HALVES):
            m_ps = ps.tile([P, PACK, P], F32, name=f"m_ps{h}", tag=f"a_then_turned{1 - h}")
            for t in range(PACK):
                nc.tensor.transpose(m_ps[:, t, :], maxima[h][:, t, :], ident[:])
            turned.append(m_ps)

        for t in range(PACK):
            nc.scalar.activation(
                out=gate[:, t, :], in_=table[t][:].indirect(idx_g[:]), func=ACT.Sigmoid,
                bias=offset[:, t : t + 1], scale=slope[:, t : t + 1],
            )

        for h in range(HALVES):
            cols = slice(h * P, (h + 1) * P)
            hid = sb.tile([P, P, PACK], BF16, name=f"hid{h}", align_bytes=64)
            nc.vector.tensor_tensor(
                hid[:], turned[h][:].rearrange("p t j -> p j t"), gate[:, :, cols].rearrange("p t j -> p j t"), ALU.mult
            )
            hid_w = sb.tile([P, P], U32, name=f"hid_w{h}", align_bytes=64)
            hid_s = sb.tile([P, P], U8, name=f"hid_s{h}", align_bytes=64)
            nc.vector.quantize_mx(hid_w[:].bitcast(E4M3), hid_s[:], hid[:].rearrange("p j t -> p (j t)"))
            for g in range(N // P):
                y_ps = ps.tile([P, P], F32, name=f"y_ps{h}{g}", tag=f"y_ps{h}{g}")
                nc.tensor.matmul_mx(
                    y_ps[:], lhsT=wb_w[:, 2 * g * P : 2 * (g + 1) * P].bitcast(E2M1),
                    lhsT_scale=wb_s[:, g * P : (g + 1) * P],
                    rhs=hid_w[:].bitcast(E4M3), rhs_scale=hid_s[:], start=True, stop=True,
                )
                y_sb = sb.tile([P, P], F32, name=f"y_sb{h}{g}")
                if h == HALVES - 1 and g == 0:
                    nc.vector.tensor_copy(y_sb[:], y_ps[:])
                    nc.sync.dma_start(out[g * P : (g + 1) * P, cols], y_sb[:])
                elif h == HALVES - 1:
                    nc.scalar.copy(y_sb[:], y_ps[:])
                    nc.scalar.dma_start(out[g * P : (g + 1) * P, cols], y_sb[:])
                else:
                    nc.scalar.copy(y_sb[:], y_ps[:])
                    nc.sync.dma_start(out[g * P : (g + 1) * P, cols], y_sb[:])
